import numpy as np
import ml_dtypes


def mxq(x, axis, fmt="e4m3"):
    dtype, down = {"e4m3": (ml_dtypes.float8_e4m3fn, 7), "e5m2": (ml_dtypes.float8_e5m2, 14)}[fmt]
    v = np.moveaxis(np.asarray(x, np.float32).astype(ml_dtypes.bfloat16).astype(np.float64), axis, -1)
    blocks = v.reshape(v.shape[:-1] + (-1, 32))
    amax = np.abs(blocks).max(-1, keepdims=True)
    byte = np.maximum(np.where(amax > 0, np.frexp(amax)[1] - 1 + 127, 0) - down, 1)
    scale = np.exp2(byte - 127.0)
    codes = (blocks / scale).astype(np.float32).astype(dtype).astype(np.float64)
    return np.moveaxis((codes * scale).reshape(v.shape), -1, axis)


WIDE = False


def mx_kscale(k):
    if not WIDE:
        return np.ones(k)
    levels = np.array([30, -30])
    if k % 512:
        return np.exp2(np.random.permutation(np.resize(levels, k // 32))).repeat(32)
    a = np.empty((k // 512, 16))
    for p in range(k // 512):
        a[p, :8] = np.random.permutation(np.resize(levels, 8))
        for g in range(8):
            far = levels[np.abs(levels - a[p, g]) >= 10]
            a[p, g + 8] = far[np.random.randint(len(far))]
    return np.exp2(a.ravel()).repeat(32)


def f64(x):
    return np.asarray(x).astype(np.float64)


def striped(idx):
    return np.tile(np.asarray(idx).reshape(-1, 16).T, (8, 1)).astype(np.uint16)


def unstriped(offs):
    return offs[:16].T.reshape(-1).astype(np.int64)


E2M1 = np.array([0.0, 0.5, 1.0, 1.5, 2.0, 3.0, 4.0, 6.0, -0.0, -0.5, -1.0, -1.5, -2.0, -3.0, -4.0, -6.0])


def pack_weight(w, fmt):
    k, n = w.shape
    w = f64(np.asarray(w, np.float32).astype(ml_dtypes.bfloat16)).reshape(k // 32, 32, n)
    amax = np.abs(w).max(1)
    if fmt == "e4m3":
        byte = np.frexp(amax)[1] - 1 + 127 - 7
    else:
        mant, ex = np.frexp(amax / 6.0)
        byte = np.where(mant > 0.5, ex, ex - 1) + 127
    byte = np.clip(np.where(amax > 0, byte, 1), 1, 254)
    scaled = (w * np.exp2(127.0 - byte)[:, None, :]).reshape(k, n).astype(np.float32)
    by_word = np.ascontiguousarray(scaled.reshape(k // 512, 128, 4, n).transpose(0, 1, 3, 2))
    if fmt == "e4m3":
        words = by_word.astype(ml_dtypes.float8_e4m3fn).view(np.uint8)
    else:
        c = by_word.astype(ml_dtypes.float4_e2m1fn).view(np.uint8) & 0xF
        words = (c[..., 0::2] | (c[..., 1::2] << 4)).reshape(k // 512, 128, 2 * n)
    return np.ascontiguousarray(words), np.ascontiguousarray(byte.astype(np.uint8).reshape(k // 512, 16, n))


def unpack_weight(words, scales, fmt):
    g, _, n = scales.shape
    words = np.ascontiguousarray(words).reshape(g, 128, n, -1)
    if fmt == "e4m3":
        vals = words.view(ml_dtypes.float8_e4m3fn).astype(np.float64)
    else:
        nib = np.empty((g, 128, n, 4), np.uint8)
        nib[..., 0::2] = words & 0xF
        nib[..., 1::2] = words >> 4
        vals = E2M1[nib]
    vals = vals * np.repeat(np.exp2(scales.astype(np.float64) - 127.0), 8, axis=1)[..., None]
    return vals.transpose(0, 1, 3, 2).reshape(g * 512, n)


K, J, T, N = 2048, 512, 512, 512


def setup_inputs():
    n = np.random.standard_normal
    idx = np.random.permutation(K)[:J]
    fk = mx_kscale(K)
    fj = mx_kscale(J)
    tj = np.ones(K)
    tj[idx] = fj
    xo = n((T, K)) * np.exp(0.5 * n((T, 1)))
    xo[:, idx] *= 4.0
    xr = xo.copy()
    xr[:, idx] = 0.0
    gbp = pack_weight(xr.T / fk[:, None], "e2m1")
    wbp = pack_weight(n((K, N)) * 1 / np.sqrt(K) * fk[:, None], "e2m1")
    wop = pack_weight(n((J, N)) * 1 / np.sqrt(J) * fj[:, None], "e4m3")
    return {
        "gb_words": gbp[0],
        "gb_scales": gbp[1],
        "wb_words": wbp[0],
        "wb_scales": wbp[1],
        "gt": (xo / tj).astype(np.float32),
        "wo_words": wop[0],
        "wo_scales": wop[1],
        "res": (1.0 * n((N, T))).astype(np.float32),
        "ls": (np.random.uniform(0.25, 1.5, (N, 1))).astype(np.float32),
        "offs": striped(idx),
    }


def reference(gb_words, gb_scales, wb_words, wb_scales, gt, wo_words, wo_scales, res, ls, offs):
    idx = unstriped(offs)
    gbu = unpack_weight(gb_words, gb_scales, "e2m1")
    wbu = unpack_weight(wb_words, wb_scales, "e2m1")
    wou = unpack_weight(wo_words, wo_scales, "e4m3")
    gl = f64(gt)[:, idx].T
    glq = mxq(gl, 0, "e5m2")
    z = wbu.T @ gbu + wou.T @ glq
    y = z * f64(ls) + f64(res)
    return y

@@ -1,0 +1,181 @@
+from contextlib import ExitStack
+
+import concourse.mybir as mybir
+from concourse.masks import make_identity
+
+F32 = mybir.dt.float32
+BF16 = mybir.dt.bfloat16
+I32 = mybir.dt.int32
+U32 = mybir.dt.uint32
+U16 = mybir.dt.uint16
+U8 = mybir.dt.uint8
+E2M1 = mybir.dt.float4_e2m1fn_x4
+E4M3 = mybir.dt.float8_e4m3fn_x4
+E5M2 = mybir.dt.float8_e5m2_x4
+MULT = mybir.AluOpType.mult
+ADD = mybir.AluOpType.add
+COPY = mybir.ActivationFunctionType.Copy
+
+K, J, T, N = 2048, 512, 512, 512
+FLOPS = 2 * N * T * (K + J)
+
+P = 128
+PASSES = K // 512
+TILES = T // P
+NT = N // P
+EARLY = T - P
+
+
+def tile_list_outlier_gradient_kernel(
+    tc, gb_words, gb_scales, wb_words, wb_scales, gt, wo_words, wo_scales, res, ls, offs, out
+):
+    nc = tc.nc
+    with ExitStack() as ctx:
+        keep = ctx.enter_context(tc.tile_pool(name="keep", bufs=1))
+        acc_pool = ctx.enter_context(tc.psum_pool(name="acc", bufs=1))
+        turn_pool = ctx.enter_context(tc.psum_pool(name="turn", bufs=2))
+
+        offsets = keep.tile([P, J // 16], U16, name="offsets")
+        wb_sc = keep.tile([P, PASSES, N], U8, name="wb_sc", align_bytes=64)
+        gb_sc = keep.tile([P, PASSES, T], U8, name="gb_sc", align_bytes=64)
+        wo_sc = keep.tile([P, 1, N], U8, name="wo_sc", align_bytes=64)
+        wb_w = keep.tile([P, PASSES, 2 * N], U8, name="wb_w", align_bytes=64)
+        gb_w = keep.tile([P, PASSES, 2 * T], U8, name="gb_w", align_bytes=64)
+        wo_w = keep.tile([P, N], U32, name="wo_w", align_bytes=64)
+        rows = [keep.tile([P, K], F32, name="rows%d" % c) for c in range(TILES)]
+        res_sb = [keep.tile([P, T], F32, name="res%d" % i) for i in range(NT)]
+        ls_rows = keep.tile([P, P], F32, name="ls_rows")
+        ls_sb = keep.tile([P, NT], F32, name="ls_sb")
+        ident = keep.tile([P, P], F32, name="ident")
+
+        nc.vector.memset(ls_rows[:], 0.0)
+        nc.vector.memset(wb_sc[:].bitcast(I32), 0)
+        nc.gpsimd.memset(gb_sc[:].bitcast(I32), 0)
+        nc.vector.memset(wo_sc[:].bitcast(I32), 0)
+
+        def load_scales(queue, plane, scales):
+            for r in range(4):
+                queue.dma_start(
+                    out=plane[r:P:32, :, :].bitcast(I32),
+                    in_=scales[:, r:16:4, :].rearrange("z q c -> q z c").bitcast(I32),
+                )
+
+        def load_words(tile, words):
+            nc.sync.dma_start(out=tile[:].bitcast(I32), in_=words.rearrange("z p c -> p z c").bitcast(I32))
+
+        def load_rows(c):
+            nc.sync.dma_start(out=rows[c][:], in_=gt[c * P : (c + 1) * P, :])
+
+        make_identity(nc, ident[:])
+        load_scales(nc.scalar, wb_sc, wb_scales)
+        load_scales(nc.scalar, gb_sc, gb_scales)
+        nc.sync.dma_start(offsets[:], offs)
+        nc.sync.dma_start(out=ls_rows[0:NT, :], in_=ls.rearrange("(i p) o -> i (p o)", p=P))
+        load_words(wb_w, wb_words)
+        load_words(gb_w, gb_words)
+        load_rows(0)
+        load_rows(1)
+        load_scales(nc.sync, wo_sc, wo_scales)
+        nc.sync.dma_start(
+            out=wo_w[:].bitcast(I32), in_=wo_words[0].rearrange("p n r -> p (n r)").bitcast(I32)
+        )
+        load_rows(2)
+        load_rows(3)
+        for i in range(NT):
+            nc.sync.dma_start(out=res_sb[i][:], in_=res[i * P : (i + 1) * P, :])
+
+        early = [acc_pool.tile([P, EARLY], F32, name="early%d" % i) for i in range(NT)]
+        late = [acc_pool.tile([P, 2, P], F32, name="late%d" % h) for h in range(NT // 2)]
+
+        def base_pass(z):
+            for i in range(NT):
+                w = wb_w[:, z, 2 * i * P : 2 * (i + 1) * P].bitcast(E2M1)
+                ws = wb_sc[:, z, i * P : (i + 1) * P]
+                spans = [
+                    (early[i][:, 0:256], 0, 256, z == 0),
+                    (early[i][:, 256:EARLY], 256, EARLY, False),
+                    (late[i // 2][:, i % 2, :], EARLY, T, z == 0 and i % 2 == 0),
+                ]
+                for acc, t0, t1, first in spans:
+                    nc.tensor.matmul_mx(
+                        out=acc,
+                        lhsT=w,
+                        lhsT_scale=ws,
+                        rhs=gb_w[:, z, 2 * t0 : 2 * t1].bitcast(E2M1),
+                        rhs_scale=gb_sc[:, z, t0:t1],
+                        start=first,
+                        stop=False,
+                    )
+
+        def quantise(c):
+            picked = keep.tile([P, J], BF16, name="picked%d" % c)
+            half = J // 2
+            nc.vector.tensor_copy(picked[:, 0:half], rows[c][:].indirect(offsets[:, 0 : half // 16]))
+            nc.scalar.activation(picked[:, half:J], rows[c][:].indirect(offsets[:, half // 16 : J // 16]), COPY)
+            words = picked[:].bitcast(F32)
+            turned = turn_pool.tile([P, 2, P], F32, name="turned")
+            for u in range(2):
+                nc.tensor.transpose(turned[:, u, :], words[:, u : J // 2 : 2], ident[:])
+            grouped = keep.tile([P, 4 * P], BF16, name="grouped%d" % c, align_bytes=64)
+            nc.scalar.copy(
+                out=grouped[:].bitcast(F32).rearrange("p (t u) -> p t u", u=2),
+                in_=turned[:].rearrange("p u t -> p t u"),
+            )
+            codes = keep.tile([P, P], U32, name="codes%d" % c, align_bytes=64)
+            scales = keep.tile([P, P], U8, name="scales%d" % c, align_bytes=64)
+            nc.vector.quantize_mx(out=codes[:].bitcast(E5M2), scales=scales[:], in_=grouped[:])
+            return codes, scales
+
+        def outlier_pass(c, codes, scales):
+            for i in range(NT):
+                if c < TILES - 1:
+                    acc = early[i][:, c * P : (c + 1) * P]
+                    last = c == TILES - 2
+                else:
+                    acc = late[i // 2][:, i % 2, :]
+                    last = i % 2 == 1
+                nc.tensor.matmul_mx(
+                    out=acc,
+                    lhsT=wo_w[:, i * P : (i + 1) * P].bitcast(E4M3),
+                    lhsT_scale=wo_sc[:, 0, i * P : (i + 1) * P],
+                    rhs=codes[:].bitcast(E5M2),
+                    rhs_scale=scales[:],
+                    start=False,
+                    stop=last,
+                )
+
+        def finish_early(i):
+            y = keep.tile([P, EARLY], F32, name="y_early%d" % i)
+            nc.vector.scalar_tensor_tensor(
+                out=y[:], in0=early[i][:], scalar=ls_sb[:, i : i + 1], in1=res_sb[i][:, 0:EARLY], op0=MULT, op1=ADD
+            )
+            nc.sync.dma_start(out=out[i * P : (i + 1) * P, 0:EARLY], in_=y[:])
+
+        def finish_late(h):
+            y = keep.tile([P, 2, P], F32, name="y_late%d" % h)
+            for s in range(2):
+                i = 2 * h + s
+                nc.vector.scalar_tensor_tensor(
+                    out=y[:, s, :],
+                    in0=late[h][:, s, :],
+                    scalar=ls_sb[:, i : i + 1],
+                    in1=res_sb[i][:, EARLY:T],
+                    op0=MULT,
+                    op1=ADD,
+                )
+            nc.sync.dma_start(
+                out=out[2 * h * P : 2 * (h + 1) * P, EARLY:T].rearrange("(s p) t -> p s t", p=P), in_=y[:]
+            )
+
+        ls_turned = turn_pool.tile([P, 2, P], F32, name="turned")
+        nc.tensor.transpose(ls_turned[:, 0, :], ls_rows[:], ident[:])
+        nc.scalar.activation(ls_sb[:], ls_turned[:, 0, 0:NT], COPY)
+        listed = [quantise(c) for c in range(TILES)]
+        for z in range(PASSES):
+            base_pass(z)
+        for c in range(TILES):
+            outlier_pass(c, *listed[c])
+        for i in range(NT):
+            finish_early(i)
+        for h in range(NT // 2):
+            finish_late(h)

@@ -24,6 +24,7 @@ PASSES = K // 512
 TILES = T // P
 NT = N // P
 EARLY = T - P
+GROUPS = ((0, 1), (2,), (3,))
 
 
 def tile_list_outlier_gradient_kernel(
@@ -39,8 +40,8 @@ def tile_list_outlier_gradient_kernel(
         wb_sc = keep.tile([P, PASSES, N], U8, name="wb_sc", align_bytes=64)
         gb_sc = keep.tile([P, PASSES, T], U8, name="gb_sc", align_bytes=64)
         wo_sc = keep.tile([P, 1, N], U8, name="wo_sc", align_bytes=64)
-        wb_w = keep.tile([P, PASSES, 2 * N], U8, name="wb_w", align_bytes=64)
-        gb_w = keep.tile([P, PASSES, 2 * T], U8, name="gb_w", align_bytes=64)
+        wb_w = [keep.tile([P, 2, 2 * N], U8, name="wb_w%d" % h, align_bytes=64) for h in range(2)]
+        gb_w = [keep.tile([P, 2, 2 * T], U8, name="gb_w%d" % h, align_bytes=64) for h in range(2)]
         wo_w = keep.tile([P, N], U32, name="wo_w", align_bytes=64)
         rows = [keep.tile([P, K], F32, name="rows%d" % c) for c in range(TILES)]
         res_sb = [keep.tile([P, T], F32, name="res%d" % i) for i in range(NT)]
@@ -48,14 +49,14 @@ def tile_list_outlier_gradient_kernel(
         ls_sb = keep.tile([P, NT], F32, name="ls_sb")
         ident = keep.tile([P, P], F32, name="ident")
 
-        nc.vector.memset(ls_rows[:], 0.0)
         nc.vector.memset(wb_sc[:].bitcast(I32), 0)
         nc.gpsimd.memset(gb_sc[:].bitcast(I32), 0)
+        nc.vector.memset(ls_rows[:], 0.0)
         nc.vector.memset(wo_sc[:].bitcast(I32), 0)
 
-        def load_scales(queue, plane, scales):
-            for r in range(4):
-                queue.dma_start(
+        def load_scales(plane, scales, which):
+            for r in which:
+                nc.sync.dma_start(
                     out=plane[r:P:32, :, :].bitcast(I32),
                     in_=scales[:, r:16:4, :].rearrange("z q c -> q z c").bitcast(I32),
                 )
@@ -67,19 +68,22 @@ def tile_list_outlier_gradient_kernel(
             nc.sync.dma_start(out=rows[c][:], in_=gt[c * P : (c + 1) * P, :])
 
         make_identity(nc, ident[:])
-        load_scales(nc.scalar, wb_sc, wb_scales)
-        load_scales(nc.scalar, gb_sc, gb_scales)
-        nc.sync.dma_start(offsets[:], offs)
-        nc.sync.dma_start(out=ls_rows[0:NT, :], in_=ls.rearrange("(i p) o -> i (p o)", p=P))
-        load_words(wb_w, wb_words)
-        load_words(gb_w, gb_words)
+        load_words(wb_w[0], wb_words[0:2])
+        load_words(gb_w[0], gb_words[0:2])
+        load_scales(wb_sc, wb_scales, range(4))
+        load_scales(gb_sc, gb_scales, range(0, 1))
         load_rows(0)
+        nc.sync.dma_start(out=ls_rows[0:NT, :], in_=ls.rearrange("(i p) o -> i (p o)", p=P))
+        load_scales(gb_sc, gb_scales, range(1, 4))
+        nc.sync.dma_start(offsets[:], offs)
         load_rows(1)
-        load_scales(nc.sync, wo_sc, wo_scales)
+        load_words(wb_w[1], wb_words[2:4])
+        load_words(gb_w[1], gb_words[2:4])
+        load_rows(2)
+        load_scales(wo_sc, wo_scales, range(4))
         nc.sync.dma_start(
             out=wo_w[:].bitcast(I32), in_=wo_words[0].rearrange("p n r -> p (n r)").bitcast(I32)
         )
-        load_rows(2)
         load_rows(3)
         for i in range(NT):
             nc.sync.dma_start(out=res_sb[i][:], in_=res[i * P : (i + 1) * P, :])
@@ -89,7 +93,7 @@ def tile_list_outlier_gradient_kernel(
 
         def base_pass(z):
             for i in range(NT):
-                w = wb_w[:, z, 2 * i * P : 2 * (i + 1) * P].bitcast(E2M1)
+                w = wb_w[z // 2][:, z % 2, 2 * i * P : 2 * (i + 1) * P].bitcast(E2M1)
                 ws = wb_sc[:, z, i * P : (i + 1) * P]
                 spans = [
                     (early[i][:, 0:256], 0, 256, z == 0),
@@ -101,81 +105,67 @@ def tile_list_outlier_gradient_kernel(
                         out=acc,
                         lhsT=w,
                         lhsT_scale=ws,
-                        rhs=gb_w[:, z, 2 * t0 : 2 * t1].bitcast(E2M1),
+                        rhs=gb_w[z // 2][:, z % 2, 2 * t0 : 2 * t1].bitcast(E2M1),
                         rhs_scale=gb_sc[:, z, t0:t1],
                         start=first,
                         stop=False,
                     )
 
-        def quantise(c):
-            picked = keep.tile([P, J], BF16, name="picked%d" % c)
-            half = J // 2
-            nc.vector.tensor_copy(picked[:, 0:half], rows[c][:].indirect(offsets[:, 0 : half // 16]))
-            nc.scalar.activation(picked[:, half:J], rows[c][:].indirect(offsets[:, half // 16 : J // 16]), COPY)
-            words = picked[:].bitcast(F32)
-            turned = turn_pool.tile([P, 2, P], F32, name="turned")
-            for u in range(2):
-                nc.tensor.transpose(turned[:, u, :], words[:, u : J // 2 : 2], ident[:])
-            grouped = keep.tile([P, 4 * P], BF16, name="grouped%d" % c, align_bytes=64)
+        def quantise(tiles):
+            width = len(tiles) * P
+            turned = turn_pool.tile([P, len(tiles), 2, P], F32, name="turned")
+            for s, c in enumerate(tiles):
+                picked = keep.tile([P, J], BF16, name="picked%d" % c)
+                half = J // 2
+                nc.vector.tensor_copy(picked[:, 0:half], rows[c][:].indirect(offsets[:, 0 : half // 16]))
+                nc.scalar.activation(picked[:, half:J], rows[c][:].indirect(offsets[:, half // 16 : J // 16]), COPY)
+                words = picked[:].bitcast(F32)
+                for u in range(2):
+                    nc.tensor.transpose(turned[:, s, u, :], words[:, u : J // 2 : 2], ident[:])
+            c = tiles[0]
+            grouped = keep.tile([P, 4 * width], BF16, name="grouped%d" % c, align_bytes=64)
             nc.scalar.copy(
-                out=grouped[:].bitcast(F32).rearrange("p (t u) -> p t u", u=2),
-                in_=turned[:].rearrange("p u t -> p t u"),
+                out=grouped[:].bitcast(F32).rearrange("p (s t u) -> p s t u", u=2, t=P),
+                in_=turned[:].rearrange("p s u t -> p s t u"),
             )
-            codes = keep.tile([P, P], U32, name="codes%d" % c, align_bytes=64)
-            scales = keep.tile([P, P], U8, name="scales%d" % c, align_bytes=64)
+            codes = keep.tile([P, width], U32, name="codes%d" % c, align_bytes=64)
+            scales = keep.tile([P, width], U8, name="scales%d" % c, align_bytes=64)
             nc.vector.quantize_mx(out=codes[:].bitcast(E5M2), scales=scales[:], in_=grouped[:])
             return codes, scales
 
-        def outlier_pass(c, codes, scales):
-            for i in range(NT):
-                if c < TILES - 1:
-                    acc = early[i][:, c * P : (c + 1) * P]
-                    last = c == TILES - 2
-                else:
-                    acc = late[i // 2][:, i % 2, :]
-                    last = i % 2 == 1
-                nc.tensor.matmul_mx(
-                    out=acc,
-                    lhsT=wo_w[:, i * P : (i + 1) * P].bitcast(E4M3),
-                    lhsT_scale=wo_sc[:, 0, i * P : (i + 1) * P],
-                    rhs=codes[:].bitcast(E5M2),
-                    rhs_scale=scales[:],
-                    start=False,
-                    stop=last,
-                )
+        def outlier_pass(tiles, i, codes, scales):
+            t0, t1 = tiles[0] * P, (tiles[-1] + 1) * P
+            if t1 < T:
+                acc, last = early[i][:, t0:t1], t1 == EARLY
+            else:
+                acc, last = late[i // 2][:, i % 2, :], i % 2 == 1
+            nc.tensor.matmul_mx(
+                out=acc,
+                lhsT=wo_w[:, i * P : (i + 1) * P].bitcast(E4M3),
+                lhsT_scale=wo_sc[:, 0, i * P : (i + 1) * P],
+                rhs=codes[:].bitcast(E5M2),
+                rhs_scale=scales[:],
+                start=False,
+                stop=last,
+            )
 
-        def finish_early(i):
-            y = keep.tile([P, EARLY], F32, name="y_early%d" % i)
+        def finish(acc, i, t0, t1):
+            y = keep.tile([P, t1 - t0], F32, name="y%d_%d" % (i, t0))
             nc.vector.scalar_tensor_tensor(
-                out=y[:], in0=early[i][:], scalar=ls_sb[:, i : i + 1], in1=res_sb[i][:, 0:EARLY], op0=MULT, op1=ADD
+                out=y[:], in0=acc, scalar=ls_sb[:, i : i + 1], in1=res_sb[i][:, t0:t1], op0=MULT, op1=ADD
             )
-            nc.sync.dma_start(out=out[i * P : (i + 1) * P, 0:EARLY], in_=y[:])
-
-        def finish_late(h):
-            y = keep.tile([P, 2, P], F32, name="y_late%d" % h)
-            for s in range(2):
-                i = 2 * h + s
-                nc.vector.scalar_tensor_tensor(
-                    out=y[:, s, :],
-                    in0=late[h][:, s, :],
-                    scalar=ls_sb[:, i : i + 1],
-                    in1=res_sb[i][:, EARLY:T],
-                    op0=MULT,
-                    op1=ADD,
-                )
-            nc.sync.dma_start(
-                out=out[2 * h * P : 2 * (h + 1) * P, EARLY:T].rearrange("(s p) t -> p s t", p=P), in_=y[:]
-            )
+            nc.sync.dma_start(out=out[i * P : (i + 1) * P, t0:t1], in_=y[:])
 
         ls_turned = turn_pool.tile([P, 2, P], F32, name="turned")
         nc.tensor.transpose(ls_turned[:, 0, :], ls_rows[:], ident[:])
         nc.scalar.activation(ls_sb[:], ls_turned[:, 0, 0:NT], COPY)
-        listed = [quantise(c) for c in range(TILES)]
+        listed = [quantise(tiles) for tiles in GROUPS]
         for z in range(PASSES):
             base_pass(z)
-        for c in range(TILES):
-            outlier_pass(c, *listed[c])
+        for tiles, operand in zip(GROUPS, listed):
+            for i in range(NT):
+                outlier_pass(tiles, i, *operand)
         for i in range(NT):
-            finish_early(i)
-        for h in range(NT // 2):
-            finish_late(h)
+            finish(early[i][:], i, 0, EARLY)
+        for i in range(NT):
+            finish(late[i // 2][:, i % 2, :], i, EARLY, T)

from contextlib import ExitStack

import concourse.mybir as mybir
from concourse.masks import make_identity

F32 = mybir.dt.float32
BF16 = mybir.dt.bfloat16
I32 = mybir.dt.int32
U32 = mybir.dt.uint32
U16 = mybir.dt.uint16
U8 = mybir.dt.uint8
E2M1 = mybir.dt.float4_e2m1fn_x4
E4M3 = mybir.dt.float8_e4m3fn_x4
E5M2 = mybir.dt.float8_e5m2_x4
MULT = mybir.AluOpType.mult
ADD = mybir.AluOpType.add
COPY = mybir.ActivationFunctionType.Copy

K, J, T, N = 2048, 512, 512, 512
FLOPS = 2 * N * T * (K + J)

P = 128
PASSES = K // 512
TILES = T // P
NT = N // P
EARLY = T - P
GROUPS = ((0, 1), (2,), (3,))


def tile_list_outlier_gradient_kernel(
    tc, gb_words, gb_scales, wb_words, wb_scales, gt, wo_words, wo_scales, res, ls, offs, out
):
    nc = tc.nc
    with ExitStack() as ctx:
        keep = ctx.enter_context(tc.tile_pool(name="keep", bufs=1))
        acc_pool = ctx.enter_context(tc.psum_pool(name="acc", bufs=1))
        turn_pool = ctx.enter_context(tc.psum_pool(name="turn", bufs=2))

        offsets = keep.tile([P, J // 16], U16, name="offsets")
        wb_sc = keep.tile([P, PASSES, N], U8, name="wb_sc", align_bytes=64)
        gb_sc = keep.tile([P, PASSES, T], U8, name="gb_sc", align_bytes=64)
        wo_sc = keep.tile([P, 1, N], U8, name="wo_sc", align_bytes=64)
        wb_w = [keep.tile([P, 2, 2 * N], U8, name="wb_w%d" % h, align_bytes=64) for h in range(2)]
        gb_w = [keep.tile([P, 2, 2 * T], U8, name="gb_w%d" % h, align_bytes=64) for h in range(2)]
        wo_w = keep.tile([P, N], U32, name="wo_w", align_bytes=64)
        rows = [keep.tile([P, K], F32, name="rows%d" % c) for c in range(TILES)]
        res_sb = [keep.tile([P, T], F32, name="res%d" % i) for i in range(NT)]
        ls_rows = keep.tile([P, P], F32, name="ls_rows")
        ls_sb = keep.tile([P, NT], F32, name="ls_sb")
        ident = keep.tile([P, P], F32, name="ident")

        nc.vector.memset(wb_sc[:].bitcast(I32), 0)
        nc.gpsimd.memset(gb_sc[:].bitcast(I32), 0)
        nc.vector.memset(ls_rows[:], 0.0)
        nc.vector.memset(wo_sc[:].bitcast(I32), 0)

        def load_scales(plane, scales, which):
            for r in which:
                nc.sync.dma_start(
                    out=plane[r:P:32, :, :].bitcast(I32),
                    in_=scales[:, r:16:4, :].rearrange("z q c -> q z c").bitcast(I32),
                )

        def load_words(tile, words):
            nc.sync.dma_start(out=tile[:].bitcast(I32), in_=words.rearrange("z p c -> p z c").bitcast(I32))

        def load_rows(c):
            nc.sync.dma_start(out=rows[c][:], in_=gt[c * P : (c + 1) * P, :])

        make_identity(nc, ident[:])
        load_words(wb_w[0], wb_words[0:2])
        load_words(gb_w[0], gb_words[0:2])
        load_scales(wb_sc, wb_scales, range(4))
        load_scales(gb_sc, gb_scales, range(0, 1))
        load_rows(0)
        nc.sync.dma_start(out=ls_rows[0:NT, :], in_=ls.rearrange("(i p) o -> i (p o)", p=P))
        load_scales(gb_sc, gb_scales, range(1, 4))
        nc.sync.dma_start(offsets[:], offs)
        load_rows(1)
        load_words(wb_w[1], wb_words[2:4])
        load_words(gb_w[1], gb_words[2:4])
        load_rows(2)
        load_scales(wo_sc, wo_scales, range(4))
        nc.sync.dma_start(
            out=wo_w[:].bitcast(I32), in_=wo_words[0].rearrange("p n r -> p (n r)").bitcast(I32)
        )
        load_rows(3)
        for i in range(NT):
            nc.sync.dma_start(out=res_sb[i][:], in_=res[i * P : (i + 1) * P, :])

        early = [acc_pool.tile([P, EARLY], F32, name="early%d" % i) for i in range(NT)]
        late = [acc_pool.tile([P, 2, P], F32, name="late%d" % h) for h in range(NT // 2)]

        def base_pass(z):
            for i in range(NT):
                w = wb_w[z // 2][:, z % 2, 2 * i * P : 2 * (i + 1) * P].bitcast(E2M1)
                ws = wb_sc[:, z, i * P : (i + 1) * P]
                spans = [
                    (early[i][:, 0:256], 0, 256, z == 0),
                    (early[i][:, 256:EARLY], 256, EARLY, False),
                    (late[i // 2][:, i % 2, :], EARLY, T, z == 0 and i % 2 == 0),
                ]
                for acc, t0, t1, first in spans:
                    nc.tensor.matmul_mx(
                        out=acc,
                        lhsT=w,
                        lhsT_scale=ws,
                        rhs=gb_w[z // 2][:, z % 2, 2 * t0 : 2 * t1].bitcast(E2M1),
                        rhs_scale=gb_sc[:, z, t0:t1],
                        start=first,
                        stop=False,
                    )

        def quantise(tiles):
            width = len(tiles) * P
            turned = turn_pool.tile([P, len(tiles), 2, P], F32, name="turned")
            for s, c in enumerate(tiles):
                picked = keep.tile([P, J], BF16, name="picked%d" % c)
                half = J // 2
                nc.vector.tensor_copy(picked[:, 0:half], rows[c][:].indirect(offsets[:, 0 : half // 16]))
                nc.scalar.activation(picked[:, half:J], rows[c][:].indirect(offsets[:, half // 16 : J // 16]), COPY)
                words = picked[:].bitcast(F32)
                for u in range(2):
                    nc.tensor.transpose(turned[:, s, u, :], words[:, u : J // 2 : 2], ident[:])
            c = tiles[0]
            grouped = keep.tile([P, 4 * width], BF16, name="grouped%d" % c, align_bytes=64)
            nc.scalar.copy(
                out=grouped[:].bitcast(F32).rearrange("p (s t u) -> p s t u", u=2, t=P),
                in_=turned[:].rearrange("p s u t -> p s t u"),
            )
            codes = keep.tile([P, width], U32, name="codes%d" % c, align_bytes=64)
            scales = keep.tile([P, width], U8, name="scales%d" % c, align_bytes=64)
            nc.vector.quantize_mx(out=codes[:].bitcast(E5M2), scales=scales[:], in_=grouped[:])
            return codes, scales

        def outlier_pass(tiles, i, codes, scales):
            t0, t1 = tiles[0] * P, (tiles[-1] + 1) * P
            if t1 < T:
                acc, last = early[i][:, t0:t1], t1 == EARLY
            else:
                acc, last = late[i // 2][:, i % 2, :], i % 2 == 1
            nc.tensor.matmul_mx(
                out=acc,
                lhsT=wo_w[:, i * P : (i + 1) * P].bitcast(E4M3),
                lhsT_scale=wo_sc[:, 0, i * P : (i + 1) * P],
                rhs=codes[:].bitcast(E5M2),
                rhs_scale=scales[:],
                start=False,
                stop=last,
            )

        def finish(acc, i, t0, t1):
            y = keep.tile([P, t1 - t0], F32, name="y%d_%d" % (i, t0))
            nc.vector.scalar_tensor_tensor(
                out=y[:], in0=acc, scalar=ls_sb[:, i : i + 1], in1=res_sb[i][:, t0:t1], op0=MULT, op1=ADD
            )
            nc.sync.dma_start(out=out[i * P : (i + 1) * P, t0:t1], in_=y[:])

        ls_turned = turn_pool.tile([P, 2, P], F32, name="turned")
        nc.tensor.transpose(ls_turned[:, 0, :], ls_rows[:], ident[:])
        nc.scalar.activation(ls_sb[:], ls_turned[:, 0, 0:NT], COPY)
        listed = [quantise(tiles) for tiles in GROUPS]
        for z in range(PASSES):
            base_pass(z)
        for tiles, operand in zip(GROUPS, listed):
            for i in range(NT):
                outlier_pass(tiles, i, *operand)
        for i in range(NT):
            finish(early[i][:], i, 0, EARLY)
        for i in range(NT):
            finish(late[i // 2][:, i % 2, :], i, EARLY, T)
